import numpy as np
import ml_dtypes


def mxq(x, axis, fmt="e4m3"):
    dtype, down = {"e4m3": (ml_dtypes.float8_e4m3fn, 7), "e5m2": (ml_dtypes.float8_e5m2, 14)}[fmt]
    v = np.moveaxis(np.asarray(x, np.float32).astype(ml_dtypes.bfloat16).astype(np.float64), axis, -1)
    blocks = v.reshape(v.shape[:-1] + (-1, 32))
    amax = np.abs(blocks).max(-1, keepdims=True)
    byte = np.maximum(np.where(amax > 0, np.frexp(amax)[1] - 1 + 127, 0) - down, 1)
    scale = np.exp2(byte - 127.0)
    codes = (blocks / scale).astype(np.float32).astype(dtype).astype(np.float64)
    return np.moveaxis((codes * scale).reshape(v.shape), -1, axis)


WIDE = False


def mx_kscale(k):
    if not WIDE:
        return np.ones(k)
    levels = np.array([10, -10, 5, -5, 0])
    if k % 512:
        return np.exp2(np.random.permutation(np.resize(levels, k // 32))).repeat(32)
    a = np.empty((k // 512, 16))
    for p in range(k // 512):
        a[p, :8] = np.random.permutation(np.resize(levels, 8))
        for g in range(8):
            far = levels[np.abs(levels - a[p, g]) >= 10]
            a[p, g + 8] = far[np.random.randint(len(far))]
    return np.exp2(a.ravel()).repeat(32)


BF16 = ml_dtypes.bfloat16


def bf(x):
    return np.asarray(x, np.float32).astype(BF16)


def f64(x):
    return np.asarray(x).astype(np.float64)


E2M1 = np.array([0.0, 0.5, 1.0, 1.5, 2.0, 3.0, 4.0, 6.0, -0.0, -0.5, -1.0, -1.5, -2.0, -3.0, -4.0, -6.0])


def pack_weight(w, fmt):
    k, n = w.shape
    w = f64(bf(w)).reshape(k // 32, 32, n)
    amax = np.abs(w).max(1)
    if fmt == "e4m3":
        byte = np.frexp(amax)[1] - 1 + 127 - 7
    else:
        mant, ex = np.frexp(amax / 6.0)
        byte = np.where(mant > 0.5, ex, ex - 1) + 127
    byte = np.clip(np.where(amax > 0, byte, 1), 1, 254)
    scaled = (w * np.exp2(127.0 - byte)[:, None, :]).reshape(k, n).astype(np.float32)
    by_word = np.ascontiguousarray(scaled.reshape(k // 512, 128, 4, n).transpose(0, 1, 3, 2))
    if fmt == "e4m3":
        words = by_word.astype(ml_dtypes.float8_e4m3fn).view(np.uint8)
    else:
        c = by_word.astype(ml_dtypes.float4_e2m1fn).view(np.uint8) & 0xF
        words = c[..., 0::2] | (c[..., 1::2] << 4)
    return np.ascontiguousarray(words), np.ascontiguousarray(byte.astype(np.uint8).reshape(k // 512, 16, n))


def unpack_weight(words, scales, fmt):
    g, p, n, _ = words.shape
    if fmt == "e4m3":
        vals = np.ascontiguousarray(words).view(ml_dtypes.float8_e4m3fn).astype(np.float64)
    else:
        nib = np.empty((g, p, n, 4), np.uint8)
        nib[..., 0::2] = words & 0xF
        nib[..., 1::2] = words >> 4
        vals = E2M1[nib]
    vals = vals * np.repeat(np.exp2(scales.astype(np.float64) - 127.0), 8, axis=1)[..., None]
    return vals.transpose(0, 1, 3, 2).reshape(g * 512, n)
def pack4(w):
    words, scales = pack_weight(w, "e2m1")
    return words.reshape(words.shape[0], 128, -1), scales


def unpack4(words, scales):
    return unpack_weight(words.reshape(words.shape[0], 128, -1, 2), scales, "e2m1")


P, D, H, O = 1024, 512, 1024, 1024


def draw0():
    a, b = mx_kscale(D), mx_kscale(H)
    s = bf(np.random.standard_normal((P, D)) * a)
    t = bf(np.random.standard_normal((P, D)) * a)
    q = bf(np.random.standard_normal((P, D)) * a)
    w_words, w_scales = pack4(np.random.standard_normal((D, H)) / np.sqrt(D) / a[:, None])
    kappa = bf(np.random.uniform(0.5, 2.0, P))
    g = bf((1.0 + 0.1 * np.random.standard_normal(H)) * b)
    v_words, v_scales = pack4(np.random.standard_normal((H, O)) / np.sqrt(H) / b[:, None])
    return {"s": s, "t": t, "q": q,
            "w_words": w_words, "w_scales": w_scales,
            "kappa": kappa,
            "g": g,
            "v_words": v_words, "v_scales": v_scales}


def core(s, t, q, w_words, w_scales, kappa, g, v_words, v_scales):
    wq = unpack4(w_words, w_scales)
    z = mxq(f64(s), 1, "e4m3") @ wq
    zx = mxq(f64(t), 1, "e4m3") @ wq
    zl = mxq(f64(q), 1, "e4m3") @ wq
    sz = np.sin(z)
    cz = np.cos(z)
    m = cz * zl + (f64(kappa)[:, None] - zx * zx) * sz
    l = f64(g)[None, :] * m
    return mxq(l, 1, "e4m3") @ unpack4(v_words, v_scales)


def e4m3fn_bytes(y):
    return np.clip(np.asarray(y, np.float64), -448.0, 448.0).astype(np.float32).astype(ml_dtypes.float8_e4m3fn).view(np.uint8)


def e4m3fn_values(b):
    return np.asarray(b, np.uint8).view(ml_dtypes.float8_e4m3fn).astype(np.float64)


def setup_inputs():
    d = draw0()
    x0 = np.asarray(d['t']).astype(np.float64)
    s = (np.max(np.abs(x0), axis=(0,), keepdims=True) / 448.0).astype(np.float32)
    out = {}
    for k, v in d.items():
        if k == 't':
            out['t_bytes'] = e4m3fn_bytes(x0 / s.astype(np.float64))
            out['t_scale'] = s
        else:
            out[k] = v
    return out


def reference(s, t_bytes, t_scale, q, w_words, w_scales, kappa, g, v_words, v_scales):
    return core(s, e4m3fn_values(t_bytes) * t_scale.astype(np.float64), q, w_words, w_scales, kappa, g, v_words, v_scales)

@@ -1,0 +1,441 @@
+import math
+from contextlib import ExitStack
+
+import concourse.mybir as mybir
+from concourse.masks import make_identity
+
+F32 = mybir.dt.float32
+BF16 = mybir.dt.bfloat16
+I32 = mybir.dt.int32
+U32 = mybir.dt.uint32
+U8 = mybir.dt.uint8
+FP8 = mybir.dt.float8_e4m3fn
+FP8X4 = mybir.dt.float8_e4m3fn_x4
+FP4X4 = mybir.dt.float4_e2m1fn_x4
+ALU = mybir.AluOpType
+ACT = mybir.ActivationFunctionType
+
+POINTS, D, H, O = 1024, 512, 1024, 1024
+FLOPS = 2 * POINTS * H * (3 * D + O)
+
+P = 128
+TILES = POINTS // P
+PAIRS = TILES // 2
+BANK = 512
+STEPS = TILES * (H // BANK)
+TWO_PI = 2.0 * math.pi
+WIDEN_V = (0, 2, 3)
+POOL_TILES = 7
+
+
+def tile_sirenhelmholtzresidual_w4_kernel(
+    tc, s, t_bytes, t_scale, q, w_words, w_scales, kappa, g, v_words, v_scales, out
+):
+    nc = tc.nc
+    with ExitStack() as ctx:
+        keep = ctx.enter_context(tc.tile_pool(name="keep", bufs=1))
+        work = ctx.enter_context(tc.tile_pool(name="work", bufs=3))
+        psum = ctx.enter_context(tc.psum_pool(name="psum", bufs=1))
+        ctx.enter_context(tc.manual_schedule())
+
+        s_rows = s.rearrange("(p i) k -> p i k", i=TILES)
+        q_rows = q.rearrange("(p i) k -> p i k", i=TILES)
+        t_rows = t_bytes.rearrange("(p i) k -> p (i k)", i=TILES)
+        out_rows = out.rearrange("(p i) n -> p i n", i=TILES)
+
+        w_code = keep.tile([P, 2 * H], U8, name="w_code", align_bytes=64)
+        w_scale = keep.tile([P, H], U8, name="w_scale", align_bytes=64)
+        v_code = keep.tile([P, 2, 2 * O], U8, name="v_code", align_bytes=64)
+        v_scale = keep.tile([P, 2, O], U8, name="v_scale", align_bytes=64)
+        ident = keep.tile([P, P], F32, name="ident")
+        tscale = keep.tile([P, 4], F32, name="tscale")
+        kap = keep.tile([P, TILES], BF16, name="kap")
+        gain = keep.tile([P, 2, 4], BF16, name="gain")
+        warm = keep.tile([P, 1], F32, name="warm")
+        warm_out = keep.tile([P, 1], F32, name="warm_out")
+
+        nc.vector.memset(w_scale[:].bitcast(I32), 0)
+        nc.vector.memset(warm[:], 0.0)
+        nc.vector.memset(v_scale[:].rearrange("p g n -> p (g n)").bitcast(I32), 0)
+        make_identity(nc, ident[:])
+
+        raw = {}
+
+        def load(name, pair):
+            if name == "t":
+                tile = keep.tile([P, 4 * D], U8, name="tbytes%d" % pair)
+                nc.sync.dma_start(out=tile[:], in_=t_rows[:, 2 * D * pair : 2 * D * (pair + 2)])
+                raw[name, pair + 1] = tile[:, 2 * D :]
+                tile = tile[:, : 2 * D]
+            else:
+                rows = s_rows if name == "s" else q_rows
+                tile = keep.tile([P, 2, D], BF16, name="%sraw%d" % (name, pair))
+                nc.sync.dma_start(out=tile[:], in_=rows[:, 2 * pair : 2 * pair + 2, :])
+            raw[name, pair] = tile
+
+        for quad in range(4):
+            nc.scalar.dma_start(
+                out=w_scale[32 * quad : 32 * quad + 4, :].bitcast(I32),
+                in_=w_scales[0, 4 * quad : 4 * quad + 4, :].bitcast(I32),
+            )
+        nc.scalar.activation(out=warm_out[:], in_=warm[:], func=ACT.Sin)
+        load("s", 0)
+        load("t", 0)
+        nc.sync.dma_start(out=w_code[:].bitcast(I32), in_=w_words[0].bitcast(I32))
+        load("q", 0)
+        nc.gpsimd.dma_start(out=tscale[:], in_=t_scale.rearrange("o (p t) -> p (o t)", t=4))
+        nc.gpsimd.dma_start(out=kap[:], in_=kappa.rearrange("(p i) -> p i", i=TILES))
+        nc.gpsimd.dma_start(out=gain[:], in_=g.rearrange("(c p t) -> p c t", p=P, t=4))
+        for name, pair in (("s", 1), ("t", 2), ("q", 1), ("s", 2), ("q", 2), ("s", 3), ("q", 3)):
+            load(name, pair)
+        for quad in range(4):
+            nc.sync.dma_start(
+                out=v_scale[32 * quad : 32 * quad + 4, :, :].bitcast(I32),
+                in_=v_scales[:, 4 * quad : 4 * quad + 4, :].rearrange("c r n -> r c n").bitcast(I32),
+            )
+        nc.sync.dma_start(out=v_code[:].bitcast(I32), in_=v_words.rearrange("c p n -> p c n").bitcast(I32))
+
+        turned = {}
+        grouped = {}
+        codes = {}
+
+        def widen(pair):
+            wide = work.tile([P, 2, D], BF16, name="wide", bufs=4)
+            copy = nc.vector.tensor_copy if pair in WIDEN_V else nc.scalar.copy
+            copy(out=wide[:].rearrange("p i k -> p (i k)"), in_=raw["t", pair][:].bitcast(FP8))
+            raw["t", pair] = wide
+
+        def turn(name, pair, tag):
+            bank = psum.tile([P, BANK], F32, name=tag, tag=tag, bufs=2)
+            for i in range(2):
+                words = raw[name, pair][:, i, :].bitcast(F32)
+                for u in range(2):
+                    col = 2 * P * u + P * i
+                    nc.tensor.transpose(bank[:, col : col + P], words[:, u : D // 2 : 2], ident[:])
+            turned[name, pair] = bank
+
+        def interleave(name, pair, on_vector=False):
+            bank = turned[name, pair]
+            tile = work.tile([P, 2 * D], BF16, name="grouped", bufs=5, align_bytes=64)
+            if name == "t":
+                nc.vector.tensor_tensor(
+                    out=tile[:].rearrange("p (n u e) -> p n u e", u=2, e=2),
+                    in0=bank[:].bitcast(BF16).rearrange("p (u n e) -> p n u e", u=2, e=2),
+                    in1=tscale[:].rearrange("p (u e) -> p u e", u=2).unsqueeze(1).to_broadcast([P, 2 * P, 2, 2]),
+                    op=ALU.mult,
+                )
+            else:
+                copy = nc.vector.tensor_copy if on_vector else nc.scalar.copy
+                copy(
+                    out=tile[:].bitcast(F32).rearrange("p (n u) -> p n u", u=2),
+                    in_=bank[:].rearrange("p (u n) -> p n u", u=2),
+                )
+            grouped[name, pair] = tile
+
+        def quantize(name, pair):
+            code = keep.tile([P, 2 * P], U32, name="%scode%d" % (name, pair), align_bytes=64)
+            scale = keep.tile([P, 2 * P], U8, name="%sscale%d" % (name, pair), align_bytes=64)
+            nc.vector.quantize_mx(out=code[:].bitcast(FP8X4), scales=scale[:], in_=grouped[name, pair][:])
+            codes[name, pair] = (code, scale)
+
+        pre = {}
+
+        def project(name, step):
+            tile_i, half = divmod(step, 2)
+            code, scale = codes[name, tile_i // 2]
+            cols = slice(P * (tile_i % 2), P * (tile_i % 2 + 1))
+            bank = psum.tile([P, BANK], F32, name="z" + name, tag="z" + name, bufs=2 if name == "s" else 1)
+            nc.tensor.matmul_mx(
+                out=bank[:],
+                lhsT=code[:, cols].bitcast(FP8X4),
+                lhsT_scale=scale[:, cols],
+                rhs=w_code[:, 2 * BANK * half : 2 * BANK * (half + 1)].bitcast(FP4X4),
+                rhs_scale=w_scale[:, BANK * half : BANK * (half + 1)],
+                start=True,
+                stop=True,
+            )
+            pre[name, step] = bank
+
+        def by_slot(bank):
+            return bank[:].rearrange("p (m t) -> p t m", t=4)
+
+        def slots(tile):
+            return tile[:].rearrange("p (t m) -> p t m", t=4)
+
+        val = {}
+
+        def new(name, step, dtype=F32, bufs=4):
+            tile = work.tile([P, BANK], dtype, name=name, tag=name, bufs=bufs)
+            val[name, step] = tile
+            return tile
+
+        def new_half(name, step):
+            tile_i, half = divmod(step, 2)
+            if half == 0:
+                val[name + "_tile", tile_i] = work.tile([P, 2 * BANK], F32, name=name, tag=name, bufs=3)
+            val[name, step] = val[name + "_tile", tile_i][:, BANK * half : BANK * (half + 1)]
+            return val[name, step]
+
+        def shift(tile_i):
+            zx2 = val["zx2_tile", tile_i]
+            shifted = work.tile([P, 2 * BANK], F32, name="shifted", bufs=2)
+            nc.gpsimd.tensor_scalar(
+                out=shifted[:], in0=zx2[:], scalar1=1.0, scalar2=kap[:, tile_i : tile_i + 1], op0=ALU.mult, op1=ALU.subtract
+            )
+            val["shifted", tile_i] = shifted
+
+        def sin_term_pool(tile_i):
+            shifted = val["shifted", tile_i]
+            new_half("sinterm", 2 * tile_i)
+            new_half("sinterm", 2 * tile_i + 1)
+            nc.gpsimd.tensor_tensor(
+                out=val["sinterm_tile", tile_i][:], in0=shifted[:], in1=val["negsin_tile", tile_i][:], op=ALU.mult
+            )
+
+        def turns(step):
+            nc.vector.tensor_scalar(
+                out=slots(new("turns", step, I32, 2)),
+                in0=by_slot(pre["s", step]),
+                scalar1=1.0 / TWO_PI,
+                scalar2=None,
+                op0=ALU.mult,
+            )
+
+        def reduce_angle(step):
+            nc.vector.scalar_tensor_tensor(
+                out=slots(new("angle", step)),
+                in0=slots(val["turns", step]),
+                scalar=-TWO_PI,
+                in1=by_slot(pre["s", step]),
+                op0=ALU.mult,
+                op1=ALU.add,
+            )
+
+        def square(step):
+            nc.scalar.activation(out=slots(new_half("zx2", step)), in_=by_slot(pre["t", step]), func=ACT.Square)
+
+        def sine(step):
+            angle = val["angle", step]
+            nc.scalar.activation(out=new_half("negsin", step)[:], in_=angle[:], func=ACT.Sin, scale=-1.0)
+
+        def magnitude(step):
+            nc.scalar.activation(out=new("absangle", step)[:], in_=val["angle", step][:], func=ACT.Abs)
+
+        def cosine(step):
+            nc.scalar.activation(
+                out=new("cos", step)[:], in_=val["absangle", step][:], func=ACT.Sin, scale=-1.0, bias=math.pi / 2
+            )
+
+        def cos_term(step):
+            nc.vector.tensor_tensor(
+                out=slots(new("costerm", step, F32, 6)),
+                in0=by_slot(pre["q", step]),
+                in1=slots(val["cos", step]),
+                op=ALU.mult,
+            )
+
+        def sin_term(step):
+            tile_i = step // 2
+            nc.vector.scalar_tensor_tensor(
+                out=new_half("sinterm", step)[:],
+                in0=val["zx2", step][:],
+                scalar=kap[:, tile_i : tile_i + 1],
+                in1=val["negsin", step][:],
+                op0=ALU.subtract,
+                op1=ALU.mult,
+            )
+
+        def residual(step):
+            bank = psum.tile([P, BANK], F32, name="m", tag="m", bufs=2)
+            for t in range(4):
+                cols = slice(P * t, P * (t + 1))
+                for n, term in enumerate(("costerm", "sinterm")):
+                    nc.tensor.matmul(
+                        bank[:, cols],
+                        lhsT=val[term, step][:, cols],
+                        rhs=ident[:],
+                        is_transpose=True,
+                        start=(n == 0),
+                        stop=(n == 1),
+                    )
+            val["m", step] = bank
+
+        def amplitude(step):
+            tile_i, half = divmod(step, 2)
+            if half == 0:
+                val["l", tile_i] = work.tile([P, 2 * BANK], BF16, name="l", tag="l", bufs=2, align_bytes=64)
+            nc.vector.tensor_tensor(
+                out=val["l", tile_i][:, BANK * half : BANK * (half + 1)].rearrange("p (n t) -> p n t", t=4),
+                in0=val["m", step][:].rearrange("p (t n) -> p n t", t=4),
+                in1=gain[:, half : half + 1, :].to_broadcast([P, P, 4]),
+                op=ALU.mult,
+            )
+
+        def quantize_l(tile_i, first=0, count=2):
+            if first == 0:
+                code = work.tile([P, 2 * P], U32, name="lcode", align_bytes=64)
+                scale = work.tile([P, 2 * P], U8, name="lscale", align_bytes=64)
+                val["lq", tile_i] = (code, scale)
+            code, scale = val["lq", tile_i]
+            cols = slice(P * first, P * (first + count))
+            nc.vector.quantize_mx(
+                out=code[:, cols].bitcast(FP8X4),
+                scales=scale[:, cols],
+                in_=val["l", tile_i][:, BANK * first : BANK * (first + count)],
+            )
+
+        def readout(step, tag="aux", passes=(0, 1)):
+            tile_i, half = divmod(step, 2)
+            code, scale = val["lq", tile_i]
+            if 0 in passes:
+                val["o", step] = psum.tile([P, BANK], F32, name=tag, tag=tag, bufs=1 if tag in ("zt", "zq") else 2)
+            bank = val["o", step]
+            for c in passes:
+                nc.tensor.matmul_mx(
+                    out=bank[:],
+                    lhsT=code[:, P * c : P * (c + 1)].bitcast(FP8X4),
+                    lhsT_scale=scale[:, P * c : P * (c + 1)],
+                    rhs=v_code[:, c, 2 * BANK * half : 2 * BANK * (half + 1)].bitcast(FP4X4),
+                    rhs_scale=v_scale[:, c, BANK * half : BANK * (half + 1)],
+                    start=(c == 0),
+                    stop=(c == 1),
+                )
+
+        def store(step, on_vector=False):
+            tile_i, half = divmod(step, 2)
+            tile = new("result", step)
+            if on_vector:
+                nc.vector.tensor_copy(out=tile[:], in_=val["o", step][:])
+            else:
+                nc.scalar.copy(out=tile[:], in_=val["o", step][:])
+            nc.sync.dma_start(out=out_rows[:, tile_i, BANK * half : BANK * (half + 1)], in_=tile[:])
+
+        widen(0)
+        turn("s", 0, "aux")
+        turn("t", 0, "m")
+        interleave("s", 0)
+        widen(1)
+        turn("q", 0, "m")
+        quantize("s", 0)
+        project("s", 0)
+        project("s", 1)
+        interleave("q", 0)
+        interleave("t", 0)
+        turns(0)
+        quantize("t", 0)
+        turn("s", 1, "aux")
+        project("t", 0)
+        interleave("s", 1)
+        reduce_angle(0)
+        sine(0)
+        magnitude(0)
+        square(0)
+        turn("t", 1, "aux")
+        project("t", 1)
+        turns(1)
+        quantize("q", 0)
+        cosine(0)
+        reduce_angle(1)
+        project("q", 0)
+        project("s", 2)
+        sine(1)
+        magnitude(1)
+        square(1)
+        project("t", 2)
+        widen(2)
+        interleave("t", 1)
+        quantize("s", 1)
+        widen(3)
+        quantize("t", 1)
+        cosine(1)
+        square(2)
+        if POOL_TILES:
+            shift(0)
+            sin_term_pool(0)
+
+        turn_at = {2: ("q", 1), 3: ("s", 2), 4: ("t", 2), 5: ("q", 2), 6: ("s", 3), 8: ("t", 3), 9: ("q", 3)}
+        quant_at = {3: [("q", 1)], 5: [("s", 2), ("t", 2)], 7: [("q", 2), ("s", 3)], 9: [("t", 3)], 11: [("q", 3)]}
+        STORE_V = ()
+        INTER_V = (2, 3)
+
+        for j in range(2, STEPS):
+            last = j == STEPS - 1
+            if j + 1 < STEPS:
+                project("s", j + 1)
+            if j == 2:
+                project("t", 3)
+            if j >= 3:
+                residual(j - 3)
+            if j in turn_at:
+                turn(*turn_at[j], "aux")
+            turns(j)
+            if j >= 4:
+                amplitude(j - 4)
+            if 3 < j + 1 < STEPS:
+                square(j + 1)
+            if j % 2 == 0 and 1 < j // 2 < POOL_TILES:
+                shift(j // 2)
+            if j >= 6 and j not in STORE_V:
+                store(j - 6)
+            if j > 2:
+                cosine(j - 1)
+            if j in turn_at and turn_at[j][0] != "t" and j not in INTER_V:
+                interleave(*turn_at[j])
+            cos_term(j - 2)
+            reduce_angle(j)
+            if last:
+                magnitude(j)
+                sine(j)
+            else:
+                sine(j)
+                magnitude(j)
+            if j == 2:
+                square(3)
+                if POOL_TILES:
+                    shift(1)
+            if j % 2 == 1 and j // 2 < POOL_TILES:
+                sin_term_pool(j // 2)
+            if j >= 5 and j % 2 == 1:
+                quantize_l((j - 5) // 2)
+            for item in quant_at.get(j, []):
+                quantize(*item)
+            if (j - 2) // 2 >= POOL_TILES:
+                sin_term(j - 2)
+            if j in turn_at and (turn_at[j][0] == "t" or j in INTER_V):
+                interleave(*turn_at[j], True)
+            if j in STORE_V:
+                store(j - 6, True)
+            project("q", j - 1)
+            if j + 2 < STEPS:
+                project("t", j + 2)
+            if j >= 5:
+                readout(j - 5)
+        cosine(15)
+        residual(13)
+        sin_term(14)
+        amplitude(12)
+        cos_term(14)
+        project("q", 15)
+        residual(14)
+        readout(11)
+        store(10)
+        sin_term(15)
+        cos_term(15)
+        amplitude(13)
+        residual(15)
+        store(11)
+        amplitude(14)
+        quantize_l(6)
+        readout(12)
+        readout(13)
+        quantize_l(7, 0, 1)
+        amplitude(15)
+        readout(14, "zs", (0,))
+        readout(15, "zt", (0,))
+        store(12)
+        quantize_l(7, 1, 1)
+        readout(14, "zs", (1,))
+        readout(15, "zt", (1,))
+        store(13)
+        store(14, True)
+        store(15)

@@ -19,75 +19,87 @@ POINTS, D, H, O = 1024, 512, 1024, 1024
 FLOPS = 2 * POINTS * H * (3 * D + O)
 
 P = 128
+PACK = 4
+BANK = 512
 TILES = POINTS // P
 PAIRS = TILES // 2
-BANK = 512
-STEPS = TILES * (H // BANK)
+HALVES = H // BANK
+STEPS = TILES * HALVES
+LAST_TILE = TILES - 1
 TWO_PI = 2.0 * math.pi
-WIDEN_V = (0, 2, 3)
-POOL_TILES = 7
+
+BANKS = {"z": 2, "zx": 1, "zl": 1, "m": 2, "aux": 2}
+PRODUCT_BANK = {"s": "z", "t": "zx", "q": "zl"}
+
+COS_LAG = 1
+COS_TERM_LAG = 2
+RESIDUAL_LAG = 3
+AMPLITUDE_LAG = 4
+READOUT_LAG = 6
 
 
 def tile_sirenhelmholtzresidual_w4_kernel(
     tc, s, t_bytes, t_scale, q, w_words, w_scales, kappa, g, v_words, v_scales, out
 ):
     nc = tc.nc
+    on_scalar = nc.scalar.copy
+    on_vector = nc.vector.tensor_copy
     with ExitStack() as ctx:
         keep = ctx.enter_context(tc.tile_pool(name="keep", bufs=1))
         work = ctx.enter_context(tc.tile_pool(name="work", bufs=3))
         psum = ctx.enter_context(tc.psum_pool(name="psum", bufs=1))
         ctx.enter_context(tc.manual_schedule())
 
-        s_rows = s.rearrange("(p i) k -> p i k", i=TILES)
-        q_rows = q.rearrange("(p i) k -> p i k", i=TILES)
-        t_rows = t_bytes.rearrange("(p i) k -> p (i k)", i=TILES)
-        out_rows = out.rearrange("(p i) n -> p i n", i=TILES)
+        def bank_of(role):
+            return psum.tile([P, BANK], F32, name=role, tag=role, bufs=BANKS[role])
 
         w_code = keep.tile([P, 2 * H], U8, name="w_code", align_bytes=64)
         w_scale = keep.tile([P, H], U8, name="w_scale", align_bytes=64)
-        v_code = keep.tile([P, 2, 2 * O], U8, name="v_code", align_bytes=64)
-        v_scale = keep.tile([P, 2, O], U8, name="v_scale", align_bytes=64)
+        v_code = keep.tile([P, HALVES, 2 * O], U8, name="v_code", align_bytes=64)
+        v_scale = keep.tile([P, HALVES, O], U8, name="v_scale", align_bytes=64)
         ident = keep.tile([P, P], F32, name="ident")
-        tscale = keep.tile([P, 4], F32, name="tscale")
-        kap = keep.tile([P, TILES], BF16, name="kap")
-        gain = keep.tile([P, 2, 4], BF16, name="gain")
-        warm = keep.tile([P, 1], F32, name="warm")
-        warm_out = keep.tile([P, 1], F32, name="warm_out")
+        t_factor = keep.tile([P, PACK], F32, name="t_factor")
+        kappa_col = keep.tile([P, TILES], BF16, name="kappa_col")
+        gain = keep.tile([P, HALVES, PACK], BF16, name="gain")
 
         nc.vector.memset(w_scale[:].bitcast(I32), 0)
-        nc.vector.memset(warm[:], 0.0)
-        nc.vector.memset(v_scale[:].rearrange("p g n -> p (g n)").bitcast(I32), 0)
+        idle = keep.tile([P, BANK], BF16, name="idle")
+        nc.vector.memset(idle[:], 0.0)
+        nc.vector.memset(v_scale[:].rearrange("p c n -> p (c n)").bitcast(I32), 0)
         make_identity(nc, ident[:])
 
-        raw = {}
+        idle_bank = bank_of("zl")
+        for repeat in range(2):
+            nc.tensor.matmul(idle_bank[:], lhsT=idle[:, :P], rhs=idle[:], start=True, stop=True)
+
+        rows = {}
 
         def load(name, pair):
-            if name == "t":
-                tile = keep.tile([P, 4 * D], U8, name="tbytes%d" % pair)
-                nc.sync.dma_start(out=tile[:], in_=t_rows[:, 2 * D * pair : 2 * D * (pair + 2)])
-                raw[name, pair + 1] = tile[:, 2 * D :]
-                tile = tile[:, : 2 * D]
-            else:
-                rows = s_rows if name == "s" else q_rows
-                tile = keep.tile([P, 2, D], BF16, name="%sraw%d" % (name, pair))
-                nc.sync.dma_start(out=tile[:], in_=rows[:, 2 * pair : 2 * pair + 2, :])
-            raw[name, pair] = tile
+            source = {"s": s, "q": q}[name].rearrange("(p i) k -> p i k", i=TILES)
+            tile = keep.tile([P, 2, D], BF16, name="%s_rows%d" % (name, pair))
+            nc.sync.dma_start(out=tile[:], in_=source[:, 2 * pair : 2 * pair + 2, :])
+            rows[name, pair] = tile
 
+        load("s", 0)
+        t_raw = keep.tile([P, TILES * D], U8, name="t_raw")
+        nc.sync.dma_start(out=t_raw[:], in_=t_bytes.rearrange("(p i) k -> p (i k)", i=TILES))
+        nc.sync.dma_start(out=w_code[:].bitcast(I32), in_=w_words[0].bitcast(I32))
+        load("q", 0)
         for quad in range(4):
             nc.scalar.dma_start(
                 out=w_scale[32 * quad : 32 * quad + 4, :].bitcast(I32),
                 in_=w_scales[0, 4 * quad : 4 * quad + 4, :].bitcast(I32),
             )
-        nc.scalar.activation(out=warm_out[:], in_=warm[:], func=ACT.Sin)
-        load("s", 0)
-        load("t", 0)
-        nc.sync.dma_start(out=w_code[:].bitcast(I32), in_=w_words[0].bitcast(I32))
-        load("q", 0)
-        nc.gpsimd.dma_start(out=tscale[:], in_=t_scale.rearrange("o (p t) -> p (o t)", t=4))
-        nc.gpsimd.dma_start(out=kap[:], in_=kappa.rearrange("(p i) -> p i", i=TILES))
-        nc.gpsimd.dma_start(out=gain[:], in_=g.rearrange("(c p t) -> p c t", p=P, t=4))
-        for name, pair in (("s", 1), ("t", 2), ("q", 1), ("s", 2), ("q", 2), ("s", 3), ("q", 3)):
-            load(name, pair)
+        idle_sine = keep.tile([P, 1], F32, name="idle_sine")
+        nc.scalar.activation(out=idle_sine[:], in_=idle[:, :1], func=ACT.Sin)
+        nc.sync.dma_start(out=t_factor[:], in_=t_scale.rearrange("o (p j) -> p (o j)", j=PACK))
+        load("s", 1)
+        load("q", 1)
+        nc.sync.dma_start(out=kappa_col[:], in_=kappa.rearrange("(p i) -> p i", i=TILES))
+        nc.sync.dma_start(out=gain[:], in_=g.rearrange("(c p j) -> p c j", p=P, j=PACK))
+        for pair in range(2, PAIRS):
+            load("s", pair)
+            load("q", pair)
         for quad in range(4):
             nc.sync.dma_start(
                 out=v_scale[32 * quad : 32 * quad + 4, :, :].bitcast(I32),
@@ -97,105 +109,89 @@ def tile_sirenhelmholtzresidual_w4_kernel(
 
         turned = {}
         grouped = {}
-        codes = {}
+        operand = {}
 
-        def widen(pair):
-            wide = work.tile([P, 2, D], BF16, name="wide", bufs=4)
-            copy = nc.vector.tensor_copy if pair in WIDEN_V else nc.scalar.copy
-            copy(out=wide[:].rearrange("p i k -> p (i k)"), in_=raw["t", pair][:].bitcast(FP8))
-            raw["t", pair] = wide
+        def widen(pair, copy):
+            tile = work.tile([P, 2, D], BF16, name="t_rows", bufs=PAIRS)
+            copy(
+                out=tile[:].rearrange("p i k -> p (i k)"),
+                in_=t_raw[:, 2 * D * pair : 2 * D * (pair + 1)].bitcast(FP8),
+            )
+            rows["t", pair] = tile
 
-        def turn(name, pair, tag):
-            bank = psum.tile([P, BANK], F32, name=tag, tag=tag, bufs=2)
+        def turn(name, pair, role):
+            bank = bank_of(role)
             for i in range(2):
-                words = raw[name, pair][:, i, :].bitcast(F32)
+                words = rows[name, pair][:, i, :].bitcast(F32)
                 for u in range(2):
                     col = 2 * P * u + P * i
                     nc.tensor.transpose(bank[:, col : col + P], words[:, u : D // 2 : 2], ident[:])
             turned[name, pair] = bank
 
-        def interleave(name, pair, on_vector=False):
-            bank = turned[name, pair]
-            tile = work.tile([P, 2 * D], BF16, name="grouped", bufs=5, align_bytes=64)
-            if name == "t":
-                nc.vector.tensor_tensor(
-                    out=tile[:].rearrange("p (n u e) -> p n u e", u=2, e=2),
-                    in0=bank[:].bitcast(BF16).rearrange("p (u n e) -> p n u e", u=2, e=2),
-                    in1=tscale[:].rearrange("p (u e) -> p u e", u=2).unsqueeze(1).to_broadcast([P, 2 * P, 2, 2]),
-                    op=ALU.mult,
-                )
-            else:
-                copy = nc.vector.tensor_copy if on_vector else nc.scalar.copy
-                copy(
-                    out=tile[:].bitcast(F32).rearrange("p (n u) -> p n u", u=2),
-                    in_=bank[:].rearrange("p (u n) -> p n u", u=2),
-                )
+        def new_grouped(name, pair):
+            tile = work.tile([P, 2 * D], BF16, name="grouped", tag="grouped", bufs=5, align_bytes=64)
             grouped[name, pair] = tile
+            return tile
+
+        def group(name, pair, copy):
+            copy(
+                out=new_grouped(name, pair)[:].bitcast(F32).rearrange("p (n u) -> p n u", u=2),
+                in_=turned[name, pair][:].rearrange("p (u n) -> p n u", u=2),
+            )
+
+        def group_t(pair):
+            nc.vector.tensor_tensor(
+                out=new_grouped("t", pair)[:].rearrange("p (n u e) -> p n u e", u=2, e=2),
+                in0=turned["t", pair][:].bitcast(BF16).rearrange("p (u n e) -> p n u e", u=2, e=2),
+                in1=t_factor[:].rearrange("p (u e) -> p u e", u=2).unsqueeze(1).to_broadcast([P, 2 * P, 2, 2]),
+                op=ALU.mult,
+            )
 
         def quantize(name, pair):
-            code = keep.tile([P, 2 * P], U32, name="%scode%d" % (name, pair), align_bytes=64)
-            scale = keep.tile([P, 2 * P], U8, name="%sscale%d" % (name, pair), align_bytes=64)
+            code = keep.tile([P, 2 * P], U32, name="%s_code%d" % (name, pair), align_bytes=64)
+            scale = keep.tile([P, 2 * P], U8, name="%s_scale%d" % (name, pair), align_bytes=64)
             nc.vector.quantize_mx(out=code[:].bitcast(FP8X4), scales=scale[:], in_=grouped[name, pair][:])
-            codes[name, pair] = (code, scale)
+            operand[name, pair] = (code, scale)
 
-        pre = {}
+        product = {}
 
-        def project(name, step):
-            tile_i, half = divmod(step, 2)
-            code, scale = codes[name, tile_i // 2]
-            cols = slice(P * (tile_i % 2), P * (tile_i % 2 + 1))
-            bank = psum.tile([P, BANK], F32, name="z" + name, tag="z" + name, bufs=2 if name == "s" else 1)
+        def project(name, step, role=None):
+            tile_i, half = divmod(step, HALVES)
+            code, scale = operand[name, tile_i // 2]
+            points = slice(P * (tile_i % 2), P * (tile_i % 2 + 1))
+            bank = bank_of(role or PRODUCT_BANK[name])
             nc.tensor.matmul_mx(
                 out=bank[:],
-                lhsT=code[:, cols].bitcast(FP8X4),
-                lhsT_scale=scale[:, cols],
+                lhsT=code[:, points].bitcast(FP8X4),
+                lhsT_scale=scale[:, points],
                 rhs=w_code[:, 2 * BANK * half : 2 * BANK * (half + 1)].bitcast(FP4X4),
                 rhs_scale=w_scale[:, BANK * half : BANK * (half + 1)],
                 start=True,
                 stop=True,
             )
-            pre[name, step] = bank
-
-        def by_slot(bank):
-            return bank[:].rearrange("p (m t) -> p t m", t=4)
-
-        def slots(tile):
-            return tile[:].rearrange("p (t m) -> p t m", t=4)
+            product[name, step] = bank[:].rearrange("n (p j) -> n j p", j=PACK)
 
         val = {}
 
-        def new(name, step, dtype=F32, bufs=4):
+        def as_jp(ap):
+            return ap.rearrange("n (j p) -> n j p", j=PACK)
+
+        def new(name, step, bufs, dtype=F32):
             tile = work.tile([P, BANK], dtype, name=name, tag=name, bufs=bufs)
-            val[name, step] = tile
-            return tile
+            val[name, step] = tile[:]
+            return tile[:]
 
         def new_half(name, step):
-            tile_i, half = divmod(step, 2)
+            tile_i, half = divmod(step, HALVES)
             if half == 0:
-                val[name + "_tile", tile_i] = work.tile([P, 2 * BANK], F32, name=name, tag=name, bufs=3)
-            val[name, step] = val[name + "_tile", tile_i][:, BANK * half : BANK * (half + 1)]
+                val[name, "tile", tile_i] = work.tile([P, H], F32, name=name, tag=name)
+            val[name, step] = val[name, "tile", tile_i][:, BANK * half : BANK * (half + 1)]
             return val[name, step]
-
-        def shift(tile_i):
-            zx2 = val["zx2_tile", tile_i]
-            shifted = work.tile([P, 2 * BANK], F32, name="shifted", bufs=2)
-            nc.gpsimd.tensor_scalar(
-                out=shifted[:], in0=zx2[:], scalar1=1.0, scalar2=kap[:, tile_i : tile_i + 1], op0=ALU.mult, op1=ALU.subtract
-            )
-            val["shifted", tile_i] = shifted
-
-        def sin_term_pool(tile_i):
-            shifted = val["shifted", tile_i]
-            new_half("sinterm", 2 * tile_i)
-            new_half("sinterm", 2 * tile_i + 1)
-            nc.gpsimd.tensor_tensor(
-                out=val["sinterm_tile", tile_i][:], in0=shifted[:], in1=val["negsin_tile", tile_i][:], op=ALU.mult
-            )
 
         def turns(step):
             nc.vector.tensor_scalar(
-                out=slots(new("turns", step, I32, 2)),
-                in0=by_slot(pre["s", step]),
+                out=as_jp(new("turns", step, 2, I32)),
+                in0=product["s", step],
                 scalar1=1.0 / TWO_PI,
                 scalar2=None,
                 op0=ALU.mult,
@@ -203,239 +199,273 @@ def tile_sirenhelmholtzresidual_w4_kernel(
 
         def reduce_angle(step):
             nc.vector.scalar_tensor_tensor(
-                out=slots(new("angle", step)),
-                in0=slots(val["turns", step]),
+                out=as_jp(new("angle", step, 4)),
+                in0=as_jp(val["turns", step]),
                 scalar=-TWO_PI,
-                in1=by_slot(pre["s", step]),
+                in1=product["s", step],
                 op0=ALU.mult,
                 op1=ALU.add,
             )
 
         def square(step):
-            nc.scalar.activation(out=slots(new_half("zx2", step)), in_=by_slot(pre["t", step]), func=ACT.Square)
+            nc.scalar.activation(out=as_jp(new_half("zx2", step)), in_=product["t", step], func=ACT.Square)
 
-        def sine(step):
-            angle = val["angle", step]
-            nc.scalar.activation(out=new_half("negsin", step)[:], in_=angle[:], func=ACT.Sin, scale=-1.0)
+        def sine(step, sign=1.0):
+            nc.scalar.activation(out=new_half("sin", step), in_=val["angle", step], func=ACT.Sin, scale=sign)
 
         def magnitude(step):
-            nc.scalar.activation(out=new("absangle", step)[:], in_=val["angle", step][:], func=ACT.Abs)
+            nc.scalar.activation(out=new("abs_angle", step, 4), in_=val["angle", step], func=ACT.Abs)
 
         def cosine(step):
             nc.scalar.activation(
-                out=new("cos", step)[:], in_=val["absangle", step][:], func=ACT.Sin, scale=-1.0, bias=math.pi / 2
+                out=new("cos", step, 4), in_=val["abs_angle", step], func=ACT.Sin, scale=-1.0, bias=math.pi / 2
             )
 
         def cos_term(step):
             nc.vector.tensor_tensor(
-                out=slots(new("costerm", step, F32, 6)),
-                in0=by_slot(pre["q", step]),
-                in1=slots(val["cos", step]),
+                out=as_jp(new("cos_term", step, 6)),
+                in0=product["q", step],
+                in1=as_jp(val["cos", step]),
                 op=ALU.mult,
             )
 
-        def sin_term(step):
-            tile_i = step // 2
+        def sin_factor(tile_i):
+            tile = work.tile([P, H], F32, name="sin_factor", bufs=2)
+            nc.gpsimd.tensor_scalar(
+                out=tile[:],
+                in0=val["zx2", "tile", tile_i][:],
+                scalar1=-1.0,
+                scalar2=kappa_col[:, tile_i : tile_i + 1],
+                op0=ALU.mult,
+                op1=ALU.add,
+            )
+            val["sin_factor", tile_i] = tile
+
+        def sin_term_of_tile(tile_i):
+            for half in range(HALVES):
+                new_half("sin_term", HALVES * tile_i + half)
+            nc.gpsimd.tensor_tensor(
+                out=val["sin_term", "tile", tile_i][:],
+                in0=val["sin_factor", tile_i][:],
+                in1=val["sin", "tile", tile_i][:],
+                op=ALU.mult,
+            )
+
+        def sin_term_of_step(step):
+            tile_i = step // HALVES
             nc.vector.scalar_tensor_tensor(
-                out=new_half("sinterm", step)[:],
-                in0=val["zx2", step][:],
-                scalar=kap[:, tile_i : tile_i + 1],
-                in1=val["negsin", step][:],
+                out=new_half("sin_term", step),
+                in0=val["zx2", step],
+                scalar=kappa_col[:, tile_i : tile_i + 1],
+                in1=val["sin", step],
                 op0=ALU.subtract,
                 op1=ALU.mult,
             )
 
-        def residual(step):
-            bank = psum.tile([P, BANK], F32, name="m", tag="m", bufs=2)
-            for t in range(4):
-                cols = slice(P * t, P * (t + 1))
-                for n, term in enumerate(("costerm", "sinterm")):
+        def residual(step, role="m"):
+            bank = bank_of(role)
+            for j in range(PACK):
+                cols = slice(P * j, P * (j + 1))
+                for term in ("cos_term", "sin_term"):
                     nc.tensor.matmul(
                         bank[:, cols],
                         lhsT=val[term, step][:, cols],
                         rhs=ident[:],
                         is_transpose=True,
-                        start=(n == 0),
-                        stop=(n == 1),
+                        start=(term == "cos_term"),
+                        stop=(term == "sin_term"),
                     )
             val["m", step] = bank
 
         def amplitude(step):
-            tile_i, half = divmod(step, 2)
+            tile_i, half = divmod(step, HALVES)
             if half == 0:
-                val["l", tile_i] = work.tile([P, 2 * BANK], BF16, name="l", tag="l", bufs=2, align_bytes=64)
+                val["l", tile_i] = work.tile([P, H], BF16, name="l", tag="l", bufs=2, align_bytes=64)
             nc.vector.tensor_tensor(
-                out=val["l", tile_i][:, BANK * half : BANK * (half + 1)].rearrange("p (n t) -> p n t", t=4),
-                in0=val["m", step][:].rearrange("p (t n) -> p n t", t=4),
-                in1=gain[:, half : half + 1, :].to_broadcast([P, P, 4]),
+                out=val["l", tile_i][:, BANK * half : BANK * (half + 1)].rearrange("p (n j) -> p n j", j=PACK),
+                in0=val["m", step][:].rearrange("p (j n) -> p n j", j=PACK),
+                in1=gain[:, half : half + 1, :].to_broadcast([P, P, PACK]),
                 op=ALU.mult,
             )
 
-        def quantize_l(tile_i, first=0, count=2):
-            if first == 0:
-                code = work.tile([P, 2 * P], U32, name="lcode", align_bytes=64)
-                scale = work.tile([P, 2 * P], U8, name="lscale", align_bytes=64)
-                val["lq", tile_i] = (code, scale)
-            code, scale = val["lq", tile_i]
-            cols = slice(P * first, P * (first + count))
+        def quantize_l(tile_i, halves=range(HALVES)):
+            if halves.start == 0:
+                code = work.tile([P, HALVES * P], U32, name="l_code", align_bytes=64)
+                scale = work.tile([P, HALVES * P], U8, name="l_scale", align_bytes=64)
+                operand["l", tile_i] = (code, scale)
+            code, scale = operand["l", tile_i]
+            cols = slice(P * halves.start, P * halves.stop)
             nc.vector.quantize_mx(
                 out=code[:, cols].bitcast(FP8X4),
                 scales=scale[:, cols],
-                in_=val["l", tile_i][:, BANK * first : BANK * (first + count)],
+                in_=val["l", tile_i][:, BANK * halves.start : BANK * halves.stop],
             )
 
-        def readout(step, tag="aux", passes=(0, 1)):
-            tile_i, half = divmod(step, 2)
-            code, scale = val["lq", tile_i]
-            if 0 in passes:
-                val["o", step] = psum.tile([P, BANK], F32, name=tag, tag=tag, bufs=1 if tag in ("zt", "zq") else 2)
-            bank = val["o", step]
-            for c in passes:
+        def readout(part, role="aux", halves=range(HALVES)):
+            tile_i, side = divmod(part, 2)
+            code, scale = operand["l", tile_i]
+            if halves.start == 0:
+                val["out", part] = bank_of(role)
+            for half in halves:
                 nc.tensor.matmul_mx(
-                    out=bank[:],
-                    lhsT=code[:, P * c : P * (c + 1)].bitcast(FP8X4),
-                    lhsT_scale=scale[:, P * c : P * (c + 1)],
-                    rhs=v_code[:, c, 2 * BANK * half : 2 * BANK * (half + 1)].bitcast(FP4X4),
-                    rhs_scale=v_scale[:, c, BANK * half : BANK * (half + 1)],
-                    start=(c == 0),
-                    stop=(c == 1),
+                    out=val["out", part][:],
+                    lhsT=code[:, P * half : P * (half + 1)].bitcast(FP8X4),
+                    lhsT_scale=scale[:, P * half : P * (half + 1)],
+                    rhs=v_code[:, half, 2 * BANK * side : 2 * BANK * (side + 1)].bitcast(FP4X4),
+                    rhs_scale=v_scale[:, half, BANK * side : BANK * (side + 1)],
+                    start=(half == 0),
+                    stop=(half == HALVES - 1),
                 )
 
-        def store(step, on_vector=False):
-            tile_i, half = divmod(step, 2)
-            tile = new("result", step)
-            if on_vector:
-                nc.vector.tensor_copy(out=tile[:], in_=val["o", step][:])
-            else:
-                nc.scalar.copy(out=tile[:], in_=val["o", step][:])
-            nc.sync.dma_start(out=out_rows[:, tile_i, BANK * half : BANK * (half + 1)], in_=tile[:])
+        out_rows = out.rearrange("(p i) n -> p i n", i=TILES)
 
-        widen(0)
+        def store(part, copy=on_scalar):
+            tile_i, side = divmod(part, 2)
+            tile = new("result", part, 6)
+            copy(out=tile, in_=val["out", part][:])
+            nc.sync.dma_start(out=out_rows[:, tile_i, BANK * side : BANK * (side + 1)], in_=tile)
+
+        widen(0, on_vector)
         turn("s", 0, "aux")
         turn("t", 0, "m")
-        interleave("s", 0)
-        widen(1)
-        turn("q", 0, "m")
+        widen(1, on_vector)
+        group("s", 0, on_scalar)
+        widen(2, on_scalar)
+        turn("q", 0, "aux")
         quantize("s", 0)
         project("s", 0)
         project("s", 1)
-        interleave("q", 0)
-        interleave("t", 0)
+        group("q", 0, on_scalar)
+        widen(3, on_scalar)
+        group_t(0)
+        for name in "sq":
+            turn(name, 1, "aux")
+        for name in "sq":
+            group(name, 1, on_scalar)
         turns(0)
         quantize("t", 0)
-        turn("s", 1, "aux")
         project("t", 0)
-        interleave("s", 1)
+        project("t", 1, "m")
+        turn("t", 1, "m")
+
+        square(0)
         reduce_angle(0)
         sine(0)
+        square(1)
+        sin_factor(0)
         magnitude(0)
-        square(0)
-        turn("t", 1, "aux")
-        project("t", 1)
+        project("t", 2)
+        project("s", 2)
         turns(1)
         quantize("q", 0)
+        square(2)
         cosine(0)
         reduce_angle(1)
-        project("q", 0)
-        project("s", 2)
         sine(1)
         magnitude(1)
-        square(1)
-        project("t", 2)
-        widen(2)
-        interleave("t", 1)
-        quantize("s", 1)
-        widen(3)
-        quantize("t", 1)
-        cosine(1)
-        square(2)
-        if POOL_TILES:
-            shift(0)
-            sin_term_pool(0)
+        sin_term_of_tile(0)
+        for name in "sq":
+            quantize(name, 1)
+        group_t(1)
+        project("q", 0)
+        project("t", 3)
 
-        turn_at = {2: ("q", 1), 3: ("s", 2), 4: ("t", 2), 5: ("q", 2), 6: ("s", 3), 8: ("t", 3), 9: ("q", 3)}
-        quant_at = {3: [("q", 1)], 5: [("s", 2), ("t", 2)], 7: [("q", 2), ("s", 3)], 9: [("t", 3)], 11: [("q", 3)]}
-        STORE_V = ()
-        INTER_V = (2, 3)
+        later_inputs = [(name, pair) for pair in range(2, PAIRS) for name in "stq"]
+        turn_at = dict(enumerate(later_inputs, start=2))
+        quantize_at = {}
+        for name, pair in later_inputs:
+            quantize_at.setdefault(4 * pair - (1 if name == "q" else 3), []).append((name, pair))
 
-        for j in range(2, STEPS):
-            last = j == STEPS - 1
-            if j + 1 < STEPS:
-                project("s", j + 1)
-            if j == 2:
-                project("t", 3)
-            if j >= 3:
-                residual(j - 3)
-            if j in turn_at:
-                turn(*turn_at[j], "aux")
-            turns(j)
-            if j >= 4:
-                amplitude(j - 4)
-            if 3 < j + 1 < STEPS:
-                square(j + 1)
-            if j % 2 == 0 and 1 < j // 2 < POOL_TILES:
-                shift(j // 2)
-            if j >= 6 and j not in STORE_V:
-                store(j - 6)
-            if j > 2:
-                cosine(j - 1)
-            if j in turn_at and turn_at[j][0] != "t" and j not in INTER_V:
-                interleave(*turn_at[j])
-            cos_term(j - 2)
-            reduce_angle(j)
-            if last:
-                magnitude(j)
-                sine(j)
-            else:
-                sine(j)
-                magnitude(j)
-            if j == 2:
-                square(3)
-                if POOL_TILES:
-                    shift(1)
-            if j % 2 == 1 and j // 2 < POOL_TILES:
-                sin_term_pool(j // 2)
-            if j >= 5 and j % 2 == 1:
-                quantize_l((j - 5) // 2)
-            for item in quant_at.get(j, []):
-                quantize(*item)
-            if (j - 2) // 2 >= POOL_TILES:
-                sin_term(j - 2)
-            if j in turn_at and (turn_at[j][0] == "t" or j in INTER_V):
-                interleave(*turn_at[j], True)
-            if j in STORE_V:
-                store(j - 6, True)
-            project("q", j - 1)
-            if j + 2 < STEPS:
-                project("t", j + 2)
-            if j >= 5:
-                readout(j - 5)
-        cosine(15)
-        residual(13)
-        sin_term(14)
-        amplitude(12)
-        cos_term(14)
-        project("q", 15)
-        residual(14)
-        readout(11)
-        store(10)
-        sin_term(15)
-        cos_term(15)
-        amplitude(13)
-        residual(15)
-        store(11)
-        amplitude(14)
-        quantize_l(6)
-        readout(12)
-        readout(13)
-        quantize_l(7, 0, 1)
-        amplitude(15)
-        readout(14, "zs", (0,))
-        readout(15, "zt", (0,))
-        store(12)
-        quantize_l(7, 1, 1)
-        readout(14, "zs", (1,))
-        readout(15, "zt", (1,))
-        store(13)
-        store(14, True)
-        store(15)
+        for step in range(2, STEPS - 2):
+            odd = step % 2 == 1
+            name, pair = turn_at.get(step, (None, None))
+            project("s", step + 1)
+            if step >= READOUT_LAG:
+                readout(step - READOUT_LAG)
+            if step >= RESIDUAL_LAG:
+                residual(step - RESIDUAL_LAG)
+            if name:
+                turn(name, pair, "aux")
+            turns(step)
+            if step == 2:
+                quantize("t", 1)
+            if step >= AMPLITUDE_LAG:
+                amplitude(step - AMPLITUDE_LAG)
+            square(step + 1)
+            if not odd:
+                sin_factor(step // 2)
+            if step >= READOUT_LAG:
+                store(step - READOUT_LAG)
+            if name in ("s", "q") and step > 2:
+                group(name, pair, on_scalar)
+            cosine(step - COS_LAG)
+            if step > 2:
+                cos_term(step - COS_TERM_LAG)
+            reduce_angle(step)
+            if step == 2:
+                cos_term(0)
+                group(name, pair, on_vector)
+            sine(step)
+            magnitude(step)
+            if odd:
+                sin_term_of_tile(step // 2)
+                if step >= READOUT_LAG - 1:
+                    quantize_l((step - READOUT_LAG + 1) // 2)
+                for item in quantize_at.get(step, []):
+                    quantize(*item)
+            if name == "t":
+                group_t(pair)
+            project("q", step - COS_TERM_LAG + 1)
+            project("t", step + 2)
+
+        a, b = STEPS - 2, STEPS - 1
+        project("s", b)
+        readout(a - 6)
+        residual(a - 3)
+        turns(a)
+        amplitude(a - 4)
+        square(b)
+        cosine(a - 1)
+        reduce_angle(a)
+        sine(a, -1.0)
+        magnitude(a)
+        turns(b)
+        cos_term(a - 2)
+        project("q", a, "zx")
+        project("q", a - 1)
+        readout(b - 6)
+        residual(a - 2)
+        reduce_angle(b)
+        magnitude(b)
+        cosine(a)
+        sine(b, -1.0)
+        cosine(b)
+        amplitude(a - 3)
+        cos_term(a - 1)
+        project("q", b)
+        residual(a - 1)
+        quantize_l(LAST_TILE - 2)
+        readout(a - 4, "z")
+        sin_term_of_step(a)
+        cos_term(a)
+        residual(a, "z")
+        readout(b - 4, "zx")
+        store(a - 6)
+        store(b - 6)
+        amplitude(a - 2)
+        sin_term_of_step(b)
+        amplitude(a - 1)
+        cos_term(b)
+        residual(b)
+        quantize_l(LAST_TILE - 1)
+        readout(a - 2)
+        readout(b - 2)
+        for half in range(HALVES):
+            amplitude(a + half)
+            quantize_l(LAST_TILE, range(half, half + 1))
+            readout(a, "m", range(half, half + 1))
+            readout(b, "zl", range(half, half + 1))
+        for part in range(a - 4, a):
+            store(part)
+        store(a, on_vector)
+        store(b)

@@ -80,11 +80,19 @@ def tile_sirenhelmholtzresidual_w4_kernel(
             nc.sync.dma_start(out=tile[:], in_=source[:, 2 * pair : 2 * pair + 2, :])
             rows[name, pair] = tile
 
+        t_raw = {}
+
+        def load_t(first):
+            tile = keep.tile([P, 4 * D], U8, name="t_raw%d" % first)
+            source = t_bytes.rearrange("(p i) k -> p (i k)", i=TILES)
+            nc.sync.dma_start(out=tile[:], in_=source[:, 2 * D * first : 2 * D * (first + 2)])
+            for n in range(2):
+                t_raw[first + n] = tile[:, 2 * D * n : 2 * D * (n + 1)]
+
+        load_t(0)
         load("s", 0)
-        t_raw = keep.tile([P, TILES * D], U8, name="t_raw")
-        nc.sync.dma_start(out=t_raw[:], in_=t_bytes.rearrange("(p i) k -> p (i k)", i=TILES))
+        load_t(2)
         nc.sync.dma_start(out=w_code[:].bitcast(I32), in_=w_words[0].bitcast(I32))
-        load("q", 0)
         for quad in range(4):
             nc.scalar.dma_start(
                 out=w_scale[32 * quad : 32 * quad + 4, :].bitcast(I32),
@@ -92,6 +100,7 @@ def tile_sirenhelmholtzresidual_w4_kernel(
             )
         idle_sine = keep.tile([P, 1], F32, name="idle_sine")
         nc.scalar.activation(out=idle_sine[:], in_=idle[:, :1], func=ACT.Sin)
+        load("q", 0)
         nc.sync.dma_start(out=t_factor[:], in_=t_scale.rearrange("o (p j) -> p (o j)", j=PACK))
         load("s", 1)
         load("q", 1)
@@ -113,10 +122,7 @@ def tile_sirenhelmholtzresidual_w4_kernel(
 
         def widen(pair, copy):
             tile = work.tile([P, 2, D], BF16, name="t_rows", bufs=PAIRS)
-            copy(
-                out=tile[:].rearrange("p i k -> p (i k)"),
-                in_=t_raw[:, 2 * D * pair : 2 * D * (pair + 1)].bitcast(FP8),
-            )
+            copy(out=tile[:].rearrange("p i k -> p (i k)"), in_=t_raw[pair].bitcast(FP8))
             rows["t", pair] = tile
 
         def turn(name, pair, role):
@@ -325,18 +331,26 @@ def tile_sirenhelmholtzresidual_w4_kernel(
             copy(out=tile, in_=val["out", part][:])
             nc.sync.dma_start(out=out_rows[:, tile_i, BANK * side : BANK * (side + 1)], in_=tile)
 
+        def store_columns(part, cols, copy):
+            tile_i, side = divmod(part, 2)
+            tile = work.tile([P, BANK // 2], F32, name="result_piece", bufs=4)
+            copy(out=tile[:], in_=val["out", part][:, cols])
+            nc.sync.dma_start(
+                out=out_rows[:, tile_i, BANK * side + cols.start : BANK * side + cols.stop], in_=tile[:]
+            )
+
         widen(0, on_vector)
         turn("s", 0, "aux")
         turn("t", 0, "m")
         widen(1, on_vector)
+        widen(2, on_vector)
         group("s", 0, on_scalar)
-        widen(2, on_scalar)
+        widen(3, on_scalar)
         turn("q", 0, "aux")
         quantize("s", 0)
         project("s", 0)
         project("s", 1)
         group("q", 0, on_scalar)
-        widen(3, on_scalar)
         group_t(0)
         for name in "sq":
             turn(name, 1, "aux")
@@ -382,10 +396,10 @@ def tile_sirenhelmholtzresidual_w4_kernel(
             project("s", step + 1)
             if step >= READOUT_LAG:
                 readout(step - READOUT_LAG)
-            if step >= RESIDUAL_LAG:
-                residual(step - RESIDUAL_LAG)
             if name:
                 turn(name, pair, "aux")
+            if step >= RESIDUAL_LAG:
+                residual(step - RESIDUAL_LAG)
             turns(step)
             if step == 2:
                 quantize("t", 1)
@@ -467,5 +481,6 @@ def tile_sirenhelmholtzresidual_w4_kernel(
             readout(b, "zl", range(half, half + 1))
         for part in range(a - 4, a):
             store(part)
-        store(a, on_vector)
-        store(b)
+        for cols in (slice(0, BANK // 2), slice(BANK // 2, BANK)):
+            store_columns(a, cols, on_vector)
+            store_columns(b, cols, on_scalar)

import math
from contextlib import ExitStack

import concourse.mybir as mybir
from concourse.masks import make_identity

F32 = mybir.dt.float32
BF16 = mybir.dt.bfloat16
I32 = mybir.dt.int32
U32 = mybir.dt.uint32
U8 = mybir.dt.uint8
FP8 = mybir.dt.float8_e4m3fn
FP8X4 = mybir.dt.float8_e4m3fn_x4
FP4X4 = mybir.dt.float4_e2m1fn_x4
ALU = mybir.AluOpType
ACT = mybir.ActivationFunctionType

POINTS, D, H, O = 1024, 512, 1024, 1024
FLOPS = 2 * POINTS * H * (3 * D + O)

P = 128
PACK = 4
BANK = 512
TILES = POINTS // P
PAIRS = TILES // 2
HALVES = H // BANK
STEPS = TILES * HALVES
LAST_TILE = TILES - 1
TWO_PI = 2.0 * math.pi

BANKS = {"z": 2, "zx": 1, "zl": 1, "m": 2, "aux": 2}
PRODUCT_BANK = {"s": "z", "t": "zx", "q": "zl"}

COS_LAG = 1
COS_TERM_LAG = 2
RESIDUAL_LAG = 3
AMPLITUDE_LAG = 4
READOUT_LAG = 6


def tile_sirenhelmholtzresidual_w4_kernel(
    tc, s, t_bytes, t_scale, q, w_words, w_scales, kappa, g, v_words, v_scales, out
):
    nc = tc.nc
    on_scalar = nc.scalar.copy
    on_vector = nc.vector.tensor_copy
    with ExitStack() as ctx:
        keep = ctx.enter_context(tc.tile_pool(name="keep", bufs=1))
        work = ctx.enter_context(tc.tile_pool(name="work", bufs=3))
        psum = ctx.enter_context(tc.psum_pool(name="psum", bufs=1))
        ctx.enter_context(tc.manual_schedule())

        def bank_of(role):
            return psum.tile([P, BANK], F32, name=role, tag=role, bufs=BANKS[role])

        w_code = keep.tile([P, 2 * H], U8, name="w_code", align_bytes=64)
        w_scale = keep.tile([P, H], U8, name="w_scale", align_bytes=64)
        v_code = keep.tile([P, HALVES, 2 * O], U8, name="v_code", align_bytes=64)
        v_scale = keep.tile([P, HALVES, O], U8, name="v_scale", align_bytes=64)
        ident = keep.tile([P, P], F32, name="ident")
        t_factor = keep.tile([P, PACK], F32, name="t_factor")
        kappa_col = keep.tile([P, TILES], BF16, name="kappa_col")
        gain = keep.tile([P, HALVES, PACK], BF16, name="gain")

        nc.vector.memset(w_scale[:].bitcast(I32), 0)
        idle = keep.tile([P, BANK], BF16, name="idle")
        nc.vector.memset(idle[:], 0.0)
        nc.vector.memset(v_scale[:].rearrange("p c n -> p (c n)").bitcast(I32), 0)
        make_identity(nc, ident[:])

        idle_bank = bank_of("zl")
        for repeat in range(2):
            nc.tensor.matmul(idle_bank[:], lhsT=idle[:, :P], rhs=idle[:], start=True, stop=True)

        rows = {}

        def load(name, pair):
            source = {"s": s, "q": q}[name].rearrange("(p i) k -> p i k", i=TILES)
            tile = keep.tile([P, 2, D], BF16, name="%s_rows%d" % (name, pair))
            nc.sync.dma_start(out=tile[:], in_=source[:, 2 * pair : 2 * pair + 2, :])
            rows[name, pair] = tile

        t_raw = {}

        def load_t(first):
            tile = keep.tile([P, 4 * D], U8, name="t_raw%d" % first)
            source = t_bytes.rearrange("(p i) k -> p (i k)", i=TILES)
            nc.sync.dma_start(out=tile[:], in_=source[:, 2 * D * first : 2 * D * (first + 2)])
            for n in range(2):
                t_raw[first + n] = tile[:, 2 * D * n : 2 * D * (n + 1)]

        load_t(0)
        load("s", 0)
        load_t(2)
        nc.sync.dma_start(out=w_code[:].bitcast(I32), in_=w_words[0].bitcast(I32))
        for quad in range(4):
            nc.scalar.dma_start(
                out=w_scale[32 * quad : 32 * quad + 4, :].bitcast(I32),
                in_=w_scales[0, 4 * quad : 4 * quad + 4, :].bitcast(I32),
            )
        idle_sine = keep.tile([P, 1], F32, name="idle_sine")
        nc.scalar.activation(out=idle_sine[:], in_=idle[:, :1], func=ACT.Sin)
        load("q", 0)
        nc.sync.dma_start(out=t_factor[:], in_=t_scale.rearrange("o (p j) -> p (o j)", j=PACK))
        load("s", 1)
        load("q", 1)
        nc.sync.dma_start(out=kappa_col[:], in_=kappa.rearrange("(p i) -> p i", i=TILES))
        nc.sync.dma_start(out=gain[:], in_=g.rearrange("(c p j) -> p c j", p=P, j=PACK))
        for pair in range(2, PAIRS):
            load("s", pair)
            load("q", pair)
        for quad in range(4):
            nc.sync.dma_start(
                out=v_scale[32 * quad : 32 * quad + 4, :, :].bitcast(I32),
                in_=v_scales[:, 4 * quad : 4 * quad + 4, :].rearrange("c r n -> r c n").bitcast(I32),
            )
        nc.sync.dma_start(out=v_code[:].bitcast(I32), in_=v_words.rearrange("c p n -> p c n").bitcast(I32))

        turned = {}
        grouped = {}
        operand = {}

        def widen(pair, copy):
            tile = work.tile([P, 2, D], BF16, name="t_rows", bufs=PAIRS)
            copy(out=tile[:].rearrange("p i k -> p (i k)"), in_=t_raw[pair].bitcast(FP8))
            rows["t", pair] = tile

        def turn(name, pair, role):
            bank = bank_of(role)
            for i in range(2):
                words = rows[name, pair][:, i, :].bitcast(F32)
                for u in range(2):
                    col = 2 * P * u + P * i
                    nc.tensor.transpose(bank[:, col : col + P], words[:, u : D // 2 : 2], ident[:])
            turned[name, pair] = bank

        def new_grouped(name, pair):
            tile = work.tile([P, 2 * D], BF16, name="grouped", tag="grouped", bufs=5, align_bytes=64)
            grouped[name, pair] = tile
            return tile

        def group(name, pair, copy):
            copy(
                out=new_grouped(name, pair)[:].bitcast(F32).rearrange("p (n u) -> p n u", u=2),
                in_=turned[name, pair][:].rearrange("p (u n) -> p n u", u=2),
            )

        def group_t(pair):
            nc.vector.tensor_tensor(
                out=new_grouped("t", pair)[:].rearrange("p (n u e) -> p n u e", u=2, e=2),
                in0=turned["t", pair][:].bitcast(BF16).rearrange("p (u n e) -> p n u e", u=2, e=2),
                in1=t_factor[:].rearrange("p (u e) -> p u e", u=2).unsqueeze(1).to_broadcast([P, 2 * P, 2, 2]),
                op=ALU.mult,
            )

        def quantize(name, pair):
            code = keep.tile([P, 2 * P], U32, name="%s_code%d" % (name, pair), align_bytes=64)
            scale = keep.tile([P, 2 * P], U8, name="%s_scale%d" % (name, pair), align_bytes=64)
            nc.vector.quantize_mx(out=code[:].bitcast(FP8X4), scales=scale[:], in_=grouped[name, pair][:])
            operand[name, pair] = (code, scale)

        product = {}

        def project(name, step, role=None):
            tile_i, half = divmod(step, HALVES)
            code, scale = operand[name, tile_i // 2]
            points = slice(P * (tile_i % 2), P * (tile_i % 2 + 1))
            bank = bank_of(role or PRODUCT_BANK[name])
            nc.tensor.matmul_mx(
                out=bank[:],
                lhsT=code[:, points].bitcast(FP8X4),
                lhsT_scale=scale[:, points],
                rhs=w_code[:, 2 * BANK * half : 2 * BANK * (half + 1)].bitcast(FP4X4),
                rhs_scale=w_scale[:, BANK * half : BANK * (half + 1)],
                start=True,
                stop=True,
            )
            product[name, step] = bank[:].rearrange("n (p j) -> n j p", j=PACK)

        val = {}

        def as_jp(ap):
            return ap.rearrange("n (j p) -> n j p", j=PACK)

        def new(name, step, bufs, dtype=F32):
            tile = work.tile([P, BANK], dtype, name=name, tag=name, bufs=bufs)
            val[name, step] = tile[:]
            return tile[:]

        def new_half(name, step):
            tile_i, half = divmod(step, HALVES)
            if half == 0:
                val[name, "tile", tile_i] = work.tile([P, H], F32, name=name, tag=name)
            val[name, step] = val[name, "tile", tile_i][:, BANK * half : BANK * (half + 1)]
            return val[name, step]

        def turns(step):
            nc.vector.tensor_scalar(
                out=as_jp(new("turns", step, 2, I32)),
                in0=product["s", step],
                scalar1=1.0 / TWO_PI,
                scalar2=None,
                op0=ALU.mult,
            )

        def reduce_angle(step):
            nc.vector.scalar_tensor_tensor(
                out=as_jp(new("angle", step, 4)),
                in0=as_jp(val["turns", step]),
                scalar=-TWO_PI,
                in1=product["s", step],
                op0=ALU.mult,
                op1=ALU.add,
            )

        def square(step):
            nc.scalar.activation(out=as_jp(new_half("zx2", step)), in_=product["t", step], func=ACT.Square)

        def sine(step, sign=1.0):
            nc.scalar.activation(out=new_half("sin", step), in_=val["angle", step], func=ACT.Sin, scale=sign)

        def magnitude(step):
            nc.scalar.activation(out=new("abs_angle", step, 4), in_=val["angle", step], func=ACT.Abs)

        def cosine(step):
            nc.scalar.activation(
                out=new("cos", step, 4), in_=val["abs_angle", step], func=ACT.Sin, scale=-1.0, bias=math.pi / 2
            )

        def cos_term(step):
            nc.vector.tensor_tensor(
                out=as_jp(new("cos_term", step, 6)),
                in0=product["q", step],
                in1=as_jp(val["cos", step]),
                op=ALU.mult,
            )

        def sin_factor(tile_i):
            tile = work.tile([P, H], F32, name="sin_factor", bufs=2)
            nc.gpsimd.tensor_scalar(
                out=tile[:],
                in0=val["zx2", "tile", tile_i][:],
                scalar1=-1.0,
                scalar2=kappa_col[:, tile_i : tile_i + 1],
                op0=ALU.mult,
                op1=ALU.add,
            )
            val["sin_factor", tile_i] = tile

        def sin_term_of_tile(tile_i):
            for half in range(HALVES):
                new_half("sin_term", HALVES * tile_i + half)
            nc.gpsimd.tensor_tensor(
                out=val["sin_term", "tile", tile_i][:],
                in0=val["sin_factor", tile_i][:],
                in1=val["sin", "tile", tile_i][:],
                op=ALU.mult,
            )

        def sin_term_of_step(step):
            tile_i = step // HALVES
            nc.vector.scalar_tensor_tensor(
                out=new_half("sin_term", step),
                in0=val["zx2", step],
                scalar=kappa_col[:, tile_i : tile_i + 1],
                in1=val["sin", step],
                op0=ALU.subtract,
                op1=ALU.mult,
            )

        def residual(step, role="m"):
            bank = bank_of(role)
            for j in range(PACK):
                cols = slice(P * j, P * (j + 1))
                for term in ("cos_term", "sin_term"):
                    nc.tensor.matmul(
                        bank[:, cols],
                        lhsT=val[term, step][:, cols],
                        rhs=ident[:],
                        is_transpose=True,
                        start=(term == "cos_term"),
                        stop=(term == "sin_term"),
                    )
            val["m", step] = bank

        def amplitude(step):
            tile_i, half = divmod(step, HALVES)
            if half == 0:
                val["l", tile_i] = work.tile([P, H], BF16, name="l", tag="l", bufs=2, align_bytes=64)
            nc.vector.tensor_tensor(
                out=val["l", tile_i][:, BANK * half : BANK * (half + 1)].rearrange("p (n j) -> p n j", j=PACK),
                in0=val["m", step][:].rearrange("p (j n) -> p n j", j=PACK),
                in1=gain[:, half : half + 1, :].to_broadcast([P, P, PACK]),
                op=ALU.mult,
            )

        def quantize_l(tile_i, halves=range(HALVES)):
            if halves.start == 0:
                code = work.tile([P, HALVES * P], U32, name="l_code", align_bytes=64)
                scale = work.tile([P, HALVES * P], U8, name="l_scale", align_bytes=64)
                operand["l", tile_i] = (code, scale)
            code, scale = operand["l", tile_i]
            cols = slice(P * halves.start, P * halves.stop)
            nc.vector.quantize_mx(
                out=code[:, cols].bitcast(FP8X4),
                scales=scale[:, cols],
                in_=val["l", tile_i][:, BANK * halves.start : BANK * halves.stop],
            )

        def readout(part, role="aux", halves=range(HALVES)):
            tile_i, side = divmod(part, 2)
            code, scale = operand["l", tile_i]
            if halves.start == 0:
                val["out", part] = bank_of(role)
            for half in halves:
                nc.tensor.matmul_mx(
                    out=val["out", part][:],
                    lhsT=code[:, P * half : P * (half + 1)].bitcast(FP8X4),
                    lhsT_scale=scale[:, P * half : P * (half + 1)],
                    rhs=v_code[:, half, 2 * BANK * side : 2 * BANK * (side + 1)].bitcast(FP4X4),
                    rhs_scale=v_scale[:, half, BANK * side : BANK * (side + 1)],
                    start=(half == 0),
                    stop=(half == HALVES - 1),
                )

        out_rows = out.rearrange("(p i) n -> p i n", i=TILES)

        def store(part, copy=on_scalar):
            tile_i, side = divmod(part, 2)
            tile = new("result", part, 6)
            copy(out=tile, in_=val["out", part][:])
            nc.sync.dma_start(out=out_rows[:, tile_i, BANK * side : BANK * (side + 1)], in_=tile)

        def store_columns(part, cols, copy):
            tile_i, side = divmod(part, 2)
            tile = work.tile([P, BANK // 2], F32, name="result_piece", bufs=4)
            copy(out=tile[:], in_=val["out", part][:, cols])
            nc.sync.dma_start(
                out=out_rows[:, tile_i, BANK * side + cols.start : BANK * side + cols.stop], in_=tile[:]
            )

        widen(0, on_vector)
        turn("s", 0, "aux")
        turn("t", 0, "m")
        widen(1, on_vector)
        widen(2, on_vector)
        group("s", 0, on_scalar)
        widen(3, on_scalar)
        turn("q", 0, "aux")
        quantize("s", 0)
        project("s", 0)
        project("s", 1)
        group("q", 0, on_scalar)
        group_t(0)
        for name in "sq":
            turn(name, 1, "aux")
        for name in "sq":
            group(name, 1, on_scalar)
        turns(0)
        quantize("t", 0)
        project("t", 0)
        project("t", 1, "m")
        turn("t", 1, "m")

        square(0)
        reduce_angle(0)
        sine(0)
        square(1)
        sin_factor(0)
        magnitude(0)
        project("t", 2)
        project("s", 2)
        turns(1)
        quantize("q", 0)
        square(2)
        cosine(0)
        reduce_angle(1)
        sine(1)
        magnitude(1)
        sin_term_of_tile(0)
        for name in "sq":
            quantize(name, 1)
        group_t(1)
        project("q", 0)
        project("t", 3)

        later_inputs = [(name, pair) for pair in range(2, PAIRS) for name in "stq"]
        turn_at = dict(enumerate(later_inputs, start=2))
        quantize_at = {}
        for name, pair in later_inputs:
            quantize_at.setdefault(4 * pair - (1 if name == "q" else 3), []).append((name, pair))

        for step in range(2, STEPS - 2):
            odd = step % 2 == 1
            name, pair = turn_at.get(step, (None, None))
            project("s", step + 1)
            if step >= READOUT_LAG:
                readout(step - READOUT_LAG)
            if name:
                turn(name, pair, "aux")
            if step >= RESIDUAL_LAG:
                residual(step - RESIDUAL_LAG)
            turns(step)
            if step == 2:
                quantize("t", 1)
            if step >= AMPLITUDE_LAG:
                amplitude(step - AMPLITUDE_LAG)
            square(step + 1)
            if not odd:
                sin_factor(step // 2)
            if step >= READOUT_LAG:
                store(step - READOUT_LAG)
            if name in ("s", "q") and step > 2:
                group(name, pair, on_scalar)
            cosine(step - COS_LAG)
            if step > 2:
                cos_term(step - COS_TERM_LAG)
            reduce_angle(step)
            if step == 2:
                cos_term(0)
                group(name, pair, on_vector)
            sine(step)
            magnitude(step)
            if odd:
                sin_term_of_tile(step // 2)
                if step >= READOUT_LAG - 1:
                    quantize_l((step - READOUT_LAG + 1) // 2)
                for item in quantize_at.get(step, []):
                    quantize(*item)
            if name == "t":
                group_t(pair)
            project("q", step - COS_TERM_LAG + 1)
            project("t", step + 2)

        a, b = STEPS - 2, STEPS - 1
        project("s", b)
        readout(a - 6)
        residual(a - 3)
        turns(a)
        amplitude(a - 4)
        square(b)
        cosine(a - 1)
        reduce_angle(a)
        sine(a, -1.0)
        magnitude(a)
        turns(b)
        cos_term(a - 2)
        project("q", a, "zx")
        project("q", a - 1)
        readout(b - 6)
        residual(a - 2)
        reduce_angle(b)
        magnitude(b)
        cosine(a)
        sine(b, -1.0)
        cosine(b)
        amplitude(a - 3)
        cos_term(a - 1)
        project("q", b)
        residual(a - 1)
        quantize_l(LAST_TILE - 2)
        readout(a - 4, "z")
        sin_term_of_step(a)
        cos_term(a)
        residual(a, "z")
        readout(b - 4, "zx")
        store(a - 6)
        store(b - 6)
        amplitude(a - 2)
        sin_term_of_step(b)
        amplitude(a - 1)
        cos_term(b)
        residual(b)
        quantize_l(LAST_TILE - 1)
        readout(a - 2)
        readout(b - 2)
        for half in range(HALVES):
            amplitude(a + half)
            quantize_l(LAST_TILE, range(half, half + 1))
            readout(a, "m", range(half, half + 1))
            readout(b, "zl", range(half, half + 1))
        for part in range(a - 4, a):
            store(part)
        for cols in (slice(0, BANK // 2), slice(BANK // 2, BANK)):
            store_columns(a, cols, on_vector)
            store_columns(b, cols, on_scalar)
